import numpy as np
import ml_dtypes


def mxq(x, axis, fmt="e4m3"):
    dtype, down = {"e4m3": (ml_dtypes.float8_e4m3fn, 7), "e5m2": (ml_dtypes.float8_e5m2, 14)}[fmt]
    v = np.moveaxis(np.asarray(x, np.float32).astype(ml_dtypes.bfloat16).astype(np.float64), axis, -1)
    blocks = v.reshape(v.shape[:-1] + (-1, 32))
    amax = np.abs(blocks).max(-1, keepdims=True)
    byte = np.maximum(np.where(amax > 0, np.frexp(amax)[1] - 1 + 127, 0) - down, 1)
    scale = np.exp2(byte - 127.0)
    codes = (blocks / scale).astype(np.float32).astype(dtype).astype(np.float64)
    return np.moveaxis((codes * scale).reshape(v.shape), -1, axis)


WIDE = False


def mx_kscale(k):
    if not WIDE:
        return np.ones(k)
    levels = np.array([30, -30])
    if k % 512:
        return np.exp2(np.random.permutation(np.resize(levels, k // 32))).repeat(32)
    a = np.empty((k // 512, 16))
    for p in range(k // 512):
        a[p, :8] = np.random.permutation(np.resize(levels, 8))
        for g in range(8):
            far = levels[np.abs(levels - a[p, g]) >= 10]
            a[p, g + 8] = far[np.random.randint(len(far))]
    return np.exp2(a.ravel()).repeat(32)


def f64(x):
    return np.asarray(x).astype(np.float64)


def striped(idx):
    return np.tile(np.asarray(idx).reshape(-1, 16).T, (8, 1)).astype(np.uint16)


def unstriped(offs):
    return offs[:16].T.reshape(-1).astype(np.int64)


E2M1 = np.array([0.0, 0.5, 1.0, 1.5, 2.0, 3.0, 4.0, 6.0, -0.0, -0.5, -1.0, -1.5, -2.0, -3.0, -4.0, -6.0])


def pack_weight(w, fmt):
    k, n = w.shape
    w = f64(np.asarray(w, np.float32).astype(ml_dtypes.bfloat16)).reshape(k // 32, 32, n)
    amax = np.abs(w).max(1)
    if fmt == "e4m3":
        byte = np.frexp(amax)[1] - 1 + 127 - 7
    else:
        mant, ex = np.frexp(amax / 6.0)
        byte = np.where(mant > 0.5, ex, ex - 1) + 127
    byte = np.clip(np.where(amax > 0, byte, 1), 1, 254)
    scaled = (w * np.exp2(127.0 - byte)[:, None, :]).reshape(k, n).astype(np.float32)
    by_word = np.ascontiguousarray(scaled.reshape(k // 512, 128, 4, n).transpose(0, 1, 3, 2))
    if fmt == "e4m3":
        words = by_word.astype(ml_dtypes.float8_e4m3fn).view(np.uint8)
    else:
        c = by_word.astype(ml_dtypes.float4_e2m1fn).view(np.uint8) & 0xF
        words = (c[..., 0::2] | (c[..., 1::2] << 4)).reshape(k // 512, 128, 2 * n)
    return np.ascontiguousarray(words), np.ascontiguousarray(byte.astype(np.uint8).reshape(k // 512, 16, n))


def unpack_weight(words, scales, fmt):
    g, _, n = scales.shape
    words = np.ascontiguousarray(words).reshape(g, 128, n, -1)
    if fmt == "e4m3":
        vals = words.view(ml_dtypes.float8_e4m3fn).astype(np.float64)
    else:
        nib = np.empty((g, 128, n, 4), np.uint8)
        nib[..., 0::2] = words & 0xF
        nib[..., 1::2] = words >> 4
        vals = E2M1[nib]
    vals = vals * np.repeat(np.exp2(scales.astype(np.float64) - 127.0), 8, axis=1)[..., None]
    return vals.transpose(0, 1, 3, 2).reshape(g * 512, n)


def bf(x):
    return np.asarray(x, np.float32).astype(ml_dtypes.bfloat16)


def planes(Y):
    r, m = Y.shape
    b = f64(bf(Y)).reshape(r // 32, 32, m)
    amax = np.abs(b).max(1)
    byte = np.clip(np.where(amax > 0, np.frexp(amax)[1] - 1 + 127 - 7, 1), 1, 254)
    codes = (b * np.exp2(127.0 - byte)[:, None, :]).reshape(r, m).astype(np.float32).astype(ml_dtypes.float8_e4m3fn).view(np.uint8)
    words = codes.reshape(r // 512, 128, 4, m).transpose(0, 1, 3, 2)
    return np.ascontiguousarray(words), np.ascontiguousarray(byte.astype(np.uint8).reshape(r // 512, 16, m))


K, T, J, B, R, O, N, C = 512, 512, 256, 32, 512, 128, 512, 1024


def setup_inputs():
    n = np.random.standard_normal
    idx = np.random.permutation(T)[:J]
    idx2 = np.random.permutation(J)[:O]
    idx3 = np.random.permutation(J)[:O]
    idx4 = np.random.permutation(C)[:O]
    fk = mx_kscale(K)
    fr = mx_kscale(R)
    wp = pack_weight(n((K, R)) * 1 / np.sqrt(K) * fk[:, None] * fr, "e4m3")
    wbp = pack_weight(n((R, N)) * 1 / np.sqrt(R) / fr[:, None], "e2m1")
    return {
        "xf": (n((K, T))).astype(np.float32),
        "fk": (np.random.uniform(0.5, 2.0, (K, 1)) / fk[:, None]).astype(np.float32),
        "w_words": wp[0],
        "w_scales": wp[1],
        "wb_words": wbp[0],
        "wb_scales": wbp[1],
        "old": (1.0 * n((N, C))).astype(np.float32),
        "offs": striped(idx),
        "offs2": striped(idx2),
        "offs3": striped(idx3),
        "offs4": striped(idx4),
    }


def reference(xf, fk, w_words, w_scales, wb_words, wb_scales, old, offs, offs2, offs3, offs4):
    idx = unstriped(offs)
    idx2 = unstriped(offs2)
    idx3 = unstriped(offs3)
    idx4 = unstriped(offs4)
    wu = unpack_weight(w_words, w_scales, "e4m3")
    wbu = unpack_weight(wb_words, wb_scales, "e2m1")
    xg = f64(xf)[:, idx]
    g1 = xg.reshape(K, B, J // B).mean(axis=2)
    g2 = np.repeat(g1, J // B, axis=1)
    u = (xg - g2) * f64(fk)
    uq = mxq(u, 0, "e4m3")
    a = wu.T @ uq
    hid = np.abs(a[:, idx2] - 0.5 * a[:, idx3])
    hidq = mxq(hid, 0, "e5m2")
    p = wbu.T @ hidq
    pp = np.zeros((N, C))
    pp[:, idx4] = p
    y = pp + 0.5 * f64(old)
    words, scales = planes(y)
    return y, words, scales

@@ -1,0 +1,221 @@
+from contextlib import ExitStack
+
+import concourse.mybir as mybir
+
+K, T, J, B, R, O, N, C = 512, 512, 256, 32, 512, 128, 512, 1024
+FLOPS = 2 * K * R * J + 2 * R * N * O
+
+F32 = mybir.dt.float32
+BF16 = mybir.dt.bfloat16
+I32 = mybir.dt.int32
+U32 = mybir.dt.uint32
+U16 = mybir.dt.uint16
+U8 = mybir.dt.uint8
+E4M3 = mybir.dt.float8_e4m3fn_x4
+E5M2 = mybir.dt.float8_e5m2_x4
+E2M1 = mybir.dt.float4_e2m1fn_x4
+ALU = mybir.AluOpType
+ACT = mybir.ActivationFunctionType
+
+P = 128
+PACK = 4
+GROUP = J // B
+U_SCALAR = 20
+CHUNK = 256
+Y_SCALAR = 32
+
+
+def tile_list_looks_centredpicks_farther_scattered_pl_kernel(
+    tc, xf, fk, w_words, w_scales, wb_words, wb_scales, old, offs, offs2, offs3, offs4, out_0, out_1, out_2
+):
+    nc = tc.nc
+    with ExitStack() as ctx:
+        lists = ctx.enter_context(tc.tile_pool(name="lists", bufs=1))
+        sb = ctx.enter_context(tc.tile_pool(name="sb", bufs=1))
+        psum = ctx.enter_context(tc.psum_pool(name="psum", bufs=1))
+
+        idx = lists.tile([P, J // 16], U16, name="idx")
+        idx2 = lists.tile([P, O // 16], U16, name="idx2")
+        idx3 = lists.tile([P, O // 16], U16, name="idx3")
+        idx4 = lists.tile([P, O // 16], U16, name="idx4")
+
+        w_scales_raw = sb.tile([P, R], U8, name="w_scales_raw", align_bytes=64)
+        wb_scales_raw = sb.tile([P, N], U8, name="wb_scales_raw", align_bytes=64)
+        nc.vector.memset(w_scales_raw[:].bitcast(I32), 0)
+        nc.gpsimd.memset(wb_scales_raw[:].bitcast(I32), 0)
+        page = [sb.tile([P, C], F32, name="page%d" % t) for t in range(PACK)]
+        for t in range(PACK):
+            nc.vector.memset(page[t][:], 0.0)
+
+        xf_rows = xf.rearrange("(p t) c -> p t c", t=PACK)
+        x = [sb.tile([P, T], F32, name="x%d" % t, tag="rows%d" % t) for t in range(PACK)]
+        factor = sb.tile([P, PACK], F32, name="factor")
+        w_raw = sb.tile([P, R], U32, name="w_raw")
+        wb_raw = sb.tile([P, 2 * N], U8, name="wb_raw")
+        old_rows = old.rearrange("(p t) c -> p t c", t=PACK)
+
+        for q in range(4):
+            nc.scalar.dma_start(
+                w_scales_raw[32 * q : 32 * q + 4, :].bitcast(I32), w_scales[0, 4 * q : 4 * q + 4, :].bitcast(I32)
+            )
+        nc.sync.dma_start(idx[:], offs)
+        for t in range(PACK):
+            nc.sync.dma_start(x[t][:], xf_rows[:, t, :])
+            if t == 0:
+                nc.sync.dma_start(factor[:], fk.rearrange("(p t) o -> p (t o)", t=PACK))
+        nc.sync.dma_start(w_raw[:].bitcast(I32), w_words[0].rearrange("p n t -> p (n t)").bitcast(I32))
+        nc.sync.dma_start(idx3[:], offs3)
+        nc.sync.dma_start(idx2[:], offs2)
+        for q in range(4):
+            nc.sync.dma_start(
+                wb_scales_raw[32 * q : 32 * q + 4, :].bitcast(I32), wb_scales[0, 4 * q : 4 * q + 4, :].bitcast(I32)
+            )
+        nc.sync.dma_start(wb_raw[:].bitcast(I32), wb_words[0].bitcast(I32))
+        nc.sync.dma_start(idx4[:], offs4)
+
+        w_planes = sb.tile([P, PACK, R // PACK], U8, name="w_planes", align_bytes=64)
+        nc.vector.tensor_copy(w_planes[:], w_scales_raw[:].rearrange("p (m t) -> p t m", t=PACK))
+
+        old_sb = []
+        u_planes = sb.tile([P, PACK, J], BF16, name="u_planes")
+        for t in range(PACK):
+            xg = sb.tile([P, J], F32, name="xg%d" % t)
+            nc.scalar.activation(xg[:], x[t][:].indirect(idx[:]), ACT.Copy)
+            old_t = sb.tile([P, C], F32, name="old%d" % t, tag="rows%d" % t)
+            nc.sync.dma_start(old_t[:], old_rows[:, t, :])
+            old_sb.append(old_t)
+            xg_groups = xg[:].rearrange("p (b i) -> p b i", i=GROUP)
+            sums = sb.tile([P, B], F32, name="sums%d" % t)
+            nc.vector.tensor_reduce(sums[:], xg_groups, mybir.AxisListType.X, ALU.add)
+            mean = sb.tile([P, B], F32, name="mean%d" % t)
+            nc.vector.tensor_scalar(mean[:], sums[:], factor[:, t : t + 1], 1.0 / GROUP, ALU.mult, ALU.mult)
+            nc.vector.scalar_tensor_tensor(
+                u_planes[:, t, :].rearrange("p (b i) -> p b i", i=GROUP),
+                xg_groups,
+                factor[:, t : t + 1],
+                mean[:].unsqueeze(2).to_broadcast([P, B, GROUP]),
+                ALU.mult,
+                ALU.subtract,
+            )
+
+        w_codes = sb.tile([P, PACK, R // PACK], U32, name="w_codes", align_bytes=64)
+        nc.vector.tensor_copy(w_codes[:], w_raw[:].rearrange("p (m t) -> p t m", t=PACK))
+
+        u_codes = sb.tile([P, J], U32, name="u_codes", align_bytes=64)
+        u_scales = sb.tile([P, J], U8, name="u_scales", align_bytes=64)
+        u_words = sb.tile([P, J, PACK], BF16, name="u_words", align_bytes=64)
+        u_dst = u_words[:].rearrange("p (c i) t -> p c t i", i=4)
+        u_src = u_planes[:].rearrange("p t (c i) -> p c t i", i=4)
+        nc.scalar.copy(u_dst[:, :U_SCALAR], u_src[:, :U_SCALAR])
+        nc.vector.tensor_copy(u_dst[:, U_SCALAR:], u_src[:, U_SCALAR:])
+        nc.vector.quantize_mx(u_codes[:].bitcast(E4M3), u_scales[:], u_words[:].rearrange("p j t -> p (j t)"))
+
+        wb_codes = sb.tile([P, 2 * N], U8, name="wb_codes", align_bytes=64)
+        nc.vector.tensor_copy(
+            wb_codes[:].bitcast(U16).rearrange("p (t m) -> p t m", t=PACK),
+            wb_raw[:].bitcast(U16).rearrange("p (m t) -> p t m", t=PACK),
+        )
+
+        wb_planes = sb.tile([P, PACK, N // PACK], U8, name="wb_planes", align_bytes=64)
+        nc.vector.tensor_copy(wb_planes[:], wb_scales_raw[:].rearrange("p (m t) -> p t m", t=PACK))
+
+        a = []
+        for t in range(PACK):
+            acc = psum.tile([P, J], F32, name="acc_a%d" % t)
+            nc.tensor.matmul_mx(
+                acc[:],
+                lhsT=w_codes[:, t, :].bitcast(E4M3),
+                lhsT_scale=w_planes[:, t, :],
+                rhs=u_codes[:].bitcast(E4M3),
+                rhs_scale=u_scales[:],
+                start=True,
+                stop=True,
+            )
+            a_t = sb.tile([P, J], F32, name="a%d" % t)
+            if t % 2 == 0:
+                nc.scalar.copy(a_t[:], acc[:])
+            else:
+                nc.vector.tensor_copy(a_t[:], acc[:])
+            a.append(a_t)
+        diff = sb.tile([P, PACK, O], F32, name="diff")
+        for t in range(PACK):
+            half = sb.tile([P, O], F32, name="half%d" % t)
+            nc.scalar.activation(half[:], a[t][:].indirect(idx3[:]), ACT.Copy, scale=-0.5)
+            nc.vector.tensor_tensor(diff[:, t, :], a[t][:].indirect(idx2[:]), half[:], ALU.add)
+        hid_words = sb.tile([P, O, PACK], BF16, name="hid_words", align_bytes=64)
+        diff_words = diff[:].rearrange("p t o -> p o t")
+        nc.scalar.activation(hid_words[:, : O // 2, :], diff_words[:, : O // 2, :], ACT.Abs)
+        nc.vector.scalar_tensor_tensor(
+            hid_words[:, O // 2 :, :], diff_words[:, O // 2 :, :], -1.0, diff_words[:, O // 2 :, :], ALU.mult, ALU.max
+        )
+        hid_codes = sb.tile([P, O], U32, name="hid_codes", align_bytes=64)
+        hid_scales = sb.tile([P, O], U8, name="hid_scales", align_bytes=64)
+        nc.vector.quantize_mx(hid_codes[:].bitcast(E5M2), hid_scales[:], hid_words[:].rearrange("p o t -> p (o t)"))
+
+        for t in range(PACK):
+            acc = psum.tile([P, O], F32, name="acc_p%d" % t)
+            nc.tensor.matmul_mx(
+                acc[:],
+                lhsT=wb_codes[:, 2 * P * t : 2 * P * (t + 1)].bitcast(E2M1),
+                lhsT_scale=wb_planes[:, t, :],
+                rhs=hid_codes[:].bitcast(E5M2),
+                rhs_scale=hid_scales[:],
+                start=True,
+                stop=True,
+            )
+            p_t = sb.tile([P, O], F32, name="p%d" % t)
+            if t == 0:
+                nc.vector.tensor_copy(p_t[:], acc[:])
+                nc.vector.tensor_copy(page[t][:].indirect(idx4[:]), p_t[:])
+            else:
+                nc.scalar.copy(p_t[:], acc[:])
+                nc.scalar.activation(page[t][:].indirect(idx4[:]), p_t[:], ACT.Copy)
+
+        chunks = C // CHUNK
+        y = [sb.tile([P, PACK, CHUNK], F32, name="y%d" % c) for c in range(chunks)]
+        out_rows = out_0.rearrange("(p t) c -> p t c", t=PACK)
+        out_words = out_1[0].rearrange("p c t -> p (c t)").bitcast(I32)
+        y_scales = sb.tile([P, C], U8, name="y_scales", align_bytes=64)
+
+        def add_pair(c, h):
+            cols = slice(c * CHUNK, (c + 1) * CHUNK)
+            for t in (2 * h, 2 * h + 1):
+                nc.vector.scalar_tensor_tensor(
+                    y[c][:, t, :], old_sb[t][:, cols], 0.5, page[t][:, cols], ALU.mult, ALU.add
+                )
+            nc.sync.dma_start(out_rows[:, 2 * h : 2 * h + 2, cols], y[c][:, 2 * h : 2 * h + 2, :])
+
+        y_words = [sb.tile([P, CHUNK, PACK], BF16, name="y_words%d" % c, align_bytes=64) for c in range(chunks)]
+
+        def weave(c):
+            dst = y_words[c][:].rearrange("p (c i) t -> p c t i", i=4)
+            src = y[c][:].rearrange("p t (c i) -> p c t i", i=4)
+            if c < chunks - 1:
+                nc.scalar.copy(dst, src)
+            else:
+                nc.scalar.copy(dst[:, :Y_SCALAR], src[:, :Y_SCALAR])
+                nc.vector.tensor_copy(dst[:, Y_SCALAR:], src[:, Y_SCALAR:])
+
+        def quantise(c):
+            cols = slice(c * CHUNK, (c + 1) * CHUNK)
+            y_codes = sb.tile([P, CHUNK], U32, name="y_codes%d" % c, align_bytes=64)
+            nc.vector.quantize_mx(
+                y_codes[:].bitcast(E4M3), y_scales[:, cols], y_words[c][:].rearrange("p c t -> p (c t)")
+            )
+            nc.sync.dma_start(out_words[:, cols], y_codes[:].bitcast(I32))
+
+        for c in range(chunks - 1):
+            add_pair(c, 0)
+        for c in range(chunks - 1):
+            add_pair(c, 1)
+            weave(c)
+        quantise(0)
+        add_pair(chunks - 1, 0)
+        add_pair(chunks - 1, 1)
+        quantise(1)
+        weave(chunks - 1)
+        quantise(2)
+        quantise(3)
+        for q in range(4):
+            queue = nc.sync if q % 2 == 0 else nc.scalar
+            queue.dma_start(out_2[0, 4 * q : 4 * q + 4, :].bitcast(I32), y_scales[32 * q : 32 * q + 4, :].bitcast(I32))

@@ -20,9 +20,8 @@ ACT = mybir.ActivationFunctionType
 P = 128
 PACK = 4
 GROUP = J // B
-U_SCALAR = 20
-CHUNK = 256
-Y_SCALAR = 32
+U_SCALAR = 28
+WIDTHS = (256, 256, 512)
 
 
 def tile_list_looks_centredpicks_farther_scattered_pl_kernel(
@@ -41,83 +40,92 @@ def tile_list_looks_centredpicks_farther_scattered_pl_kernel(
 
         w_scales_raw = sb.tile([P, R], U8, name="w_scales_raw", align_bytes=64)
         wb_scales_raw = sb.tile([P, N], U8, name="wb_scales_raw", align_bytes=64)
-        nc.vector.memset(w_scales_raw[:].bitcast(I32), 0)
+        nc.gpsimd.memset(w_scales_raw[:].bitcast(I32), 0)
         nc.gpsimd.memset(wb_scales_raw[:].bitcast(I32), 0)
+        warm = sb.tile([P, 2], F32, name="warm")
+        nc.gpsimd.memset(warm[:, 0:1], 0.0)
+        nc.scalar.activation(warm[:, 1:2], warm[:, 0:1], ACT.Abs)
         page = [sb.tile([P, C], F32, name="page%d" % t) for t in range(PACK)]
-        for t in range(PACK):
+        for t in range(PACK - 1):
             nc.vector.memset(page[t][:], 0.0)
 
         xf_rows = xf.rearrange("(p t) c -> p t c", t=PACK)
-        x = [sb.tile([P, T], F32, name="x%d" % t, tag="rows%d" % t) for t in range(PACK)]
+        x = [sb.tile([P, T], F32, name="x%d" % t, tag="tokens%d" % t) for t in range(PACK)]
         factor = sb.tile([P, PACK], F32, name="factor")
         w_raw = sb.tile([P, R], U32, name="w_raw")
-        wb_raw = sb.tile([P, 2 * N], U8, name="wb_raw")
+        wb_raw = sb.tile([P, 2 * N], U8, name="wb_raw", tag="undealt_b", align_bytes=64)
         old_rows = old.rearrange("(p t) c -> p t c", t=PACK)
 
-        for q in range(4):
-            nc.scalar.dma_start(
-                w_scales_raw[32 * q : 32 * q + 4, :].bitcast(I32), w_scales[0, 4 * q : 4 * q + 4, :].bitcast(I32)
-            )
-        nc.sync.dma_start(idx[:], offs)
         for t in range(PACK):
             nc.sync.dma_start(x[t][:], xf_rows[:, t, :])
             if t == 0:
+                nc.sync.dma_start(idx[:], offs)
                 nc.sync.dma_start(factor[:], fk.rearrange("(p t) o -> p (t o)", t=PACK))
         nc.sync.dma_start(w_raw[:].bitcast(I32), w_words[0].rearrange("p n t -> p (n t)").bitcast(I32))
-        nc.sync.dma_start(idx3[:], offs3)
-        nc.sync.dma_start(idx2[:], offs2)
+        for q in range(4):
+            nc.sync.dma_start(
+                w_scales_raw[32 * q : 32 * q + 4, :].bitcast(I32), w_scales[0, 4 * q : 4 * q + 4, :].bitcast(I32)
+            )
+        nc.sync.dma_start(wb_raw[:].bitcast(I32), wb_words[0].bitcast(I32))
         for q in range(4):
             nc.sync.dma_start(
                 wb_scales_raw[32 * q : 32 * q + 4, :].bitcast(I32), wb_scales[0, 4 * q : 4 * q + 4, :].bitcast(I32)
             )
-        nc.sync.dma_start(wb_raw[:].bitcast(I32), wb_words[0].bitcast(I32))
+        nc.gpsimd.memset(page[PACK - 1][:], 0.0)
+        nc.sync.dma_start(idx3[:], offs3)
+        nc.sync.dma_start(idx2[:], offs2)
         nc.sync.dma_start(idx4[:], offs4)
-
-        w_planes = sb.tile([P, PACK, R // PACK], U8, name="w_planes", align_bytes=64)
-        nc.vector.tensor_copy(w_planes[:], w_scales_raw[:].rearrange("p (m t) -> p t m", t=PACK))
-
-        old_sb = []
-        u_planes = sb.tile([P, PACK, J], BF16, name="u_planes")
+        old_sb = [sb.tile([P, C], F32, name="old%d" % t) for t in range(PACK)]
         for t in range(PACK):
-            xg = sb.tile([P, J], F32, name="xg%d" % t)
-            nc.scalar.activation(xg[:], x[t][:].indirect(idx[:]), ACT.Copy)
-            old_t = sb.tile([P, C], F32, name="old%d" % t, tag="rows%d" % t)
-            nc.sync.dma_start(old_t[:], old_rows[:, t, :])
-            old_sb.append(old_t)
-            xg_groups = xg[:].rearrange("p (b i) -> p b i", i=GROUP)
+            nc.sync.dma_start(old_sb[t][:], old_rows[:, t, :])
+
+        centred = []
+        for t in range(PACK):
+            xg = sb.tile([P, B, GROUP], F32, name="xg%d" % t, tag="picked%d" % t, align_bytes=64)
+            nc.scalar.activation(xg[:].rearrange("p b i -> p (b i)"), x[t][:].indirect(idx[:]), ACT.Copy)
             sums = sb.tile([P, B], F32, name="sums%d" % t)
-            nc.vector.tensor_reduce(sums[:], xg_groups, mybir.AxisListType.X, ALU.add)
-            mean = sb.tile([P, B], F32, name="mean%d" % t)
-            nc.vector.tensor_scalar(mean[:], sums[:], factor[:, t : t + 1], 1.0 / GROUP, ALU.mult, ALU.mult)
+            nc.vector.tensor_reduce(sums[:], xg[:], mybir.AxisListType.X, ALU.add)
+            centred_t = sb.tile([P, B, GROUP], F32, name="centred%d" % t)
             nc.vector.scalar_tensor_tensor(
-                u_planes[:, t, :].rearrange("p (b i) -> p b i", i=GROUP),
-                xg_groups,
-                factor[:, t : t + 1],
-                mean[:].unsqueeze(2).to_broadcast([P, B, GROUP]),
-                ALU.mult,
-                ALU.subtract,
+                centred_t[:], sums[:].unsqueeze(2).to_broadcast([P, B, GROUP]), -1.0 / GROUP, xg[:], ALU.mult, ALU.add
+            )
+            centred.append(centred_t)
+        u_planes = sb.tile([P, PACK, J], BF16, name="u_planes", tag="tokens%d" % (PACK - 1))
+        for t in range(PACK):
+            nc.scalar.activation(
+                u_planes[:, t, :], centred[t][:].rearrange("p b i -> p (b i)"), ACT.Copy, scale=factor[:, t : t + 1]
             )
 
-        w_codes = sb.tile([P, PACK, R // PACK], U32, name="w_codes", align_bytes=64)
-        nc.vector.tensor_copy(w_codes[:], w_raw[:].rearrange("p (m t) -> p t m", t=PACK))
+        w_codes = sb.tile([P, PACK, R // PACK], U32, name="w_codes", tag="picked%d" % (PACK - 2), align_bytes=64)
+        nc.vector.tensor_copy(
+            w_codes[:].rearrange("p t (m i) -> p m t i", i=4), w_raw[:].rearrange("p (m i t) -> p m t i", i=4, t=PACK)
+        )
 
+        w_planes = sb.tile([P, PACK, R // PACK], U8, name="w_planes", tag="picked%d" % (PACK - 1), align_bytes=64)
+        nc.vector.tensor_copy(
+            w_planes[:].rearrange("p t (m i) -> p m t i", i=16),
+            w_scales_raw[:].rearrange("p (m i t) -> p m t i", i=16, t=PACK),
+        )
         u_codes = sb.tile([P, J], U32, name="u_codes", align_bytes=64)
         u_scales = sb.tile([P, J], U8, name="u_scales", align_bytes=64)
-        u_words = sb.tile([P, J, PACK], BF16, name="u_words", align_bytes=64)
+        u_words = sb.tile([P, J, PACK], BF16, name="u_words", tag="woven", align_bytes=64)
         u_dst = u_words[:].rearrange("p (c i) t -> p c t i", i=4)
         u_src = u_planes[:].rearrange("p t (c i) -> p c t i", i=4)
         nc.scalar.copy(u_dst[:, :U_SCALAR], u_src[:, :U_SCALAR])
         nc.vector.tensor_copy(u_dst[:, U_SCALAR:], u_src[:, U_SCALAR:])
         nc.vector.quantize_mx(u_codes[:].bitcast(E4M3), u_scales[:], u_words[:].rearrange("p j t -> p (j t)"))
 
-        wb_codes = sb.tile([P, 2 * N], U8, name="wb_codes", align_bytes=64)
+        wb_codes = sb.tile([P, 2 * N], U8, name="wb_codes", tag="woven", align_bytes=64)
         nc.vector.tensor_copy(
-            wb_codes[:].bitcast(U16).rearrange("p (t m) -> p t m", t=PACK),
-            wb_raw[:].bitcast(U16).rearrange("p (m t) -> p t m", t=PACK),
+            wb_codes[:].bitcast(U16).rearrange("p (t m i) -> p m t i", t=PACK, i=8),
+            wb_raw[:].bitcast(U16).rearrange("p (m i t) -> p m t i", t=PACK, i=8),
         )
 
-        wb_planes = sb.tile([P, PACK, N // PACK], U8, name="wb_planes", align_bytes=64)
-        nc.vector.tensor_copy(wb_planes[:], wb_scales_raw[:].rearrange("p (m t) -> p t m", t=PACK))
+        wb_planes = sb.tile([P, PACK, N // PACK], U8, name="wb_planes", tag="undealt_b", align_bytes=64)
+        nc.vector.tensor_copy(
+            wb_planes[:].rearrange("p t (m i) -> p m t i", i=16),
+            wb_scales_raw[:].rearrange("p (m i t) -> p m t i", i=16, t=PACK),
+        )
 
         a = []
         for t in range(PACK):
@@ -144,78 +152,82 @@ def tile_list_looks_centredpicks_farther_scattered_pl_kernel(
             nc.vector.tensor_tensor(diff[:, t, :], a[t][:].indirect(idx2[:]), half[:], ALU.add)
         hid_words = sb.tile([P, O, PACK], BF16, name="hid_words", align_bytes=64)
         diff_words = diff[:].rearrange("p t o -> p o t")
-        nc.scalar.activation(hid_words[:, : O // 2, :], diff_words[:, : O // 2, :], ACT.Abs)
-        nc.vector.scalar_tensor_tensor(
-            hid_words[:, O // 2 :, :], diff_words[:, O // 2 :, :], -1.0, diff_words[:, O // 2 :, :], ALU.mult, ALU.max
-        )
+        for h in range(2):
+            pair = slice(2 * h, 2 * h + 2)
+            nc.scalar.activation(hid_words[:, :, pair], diff_words[:, :, pair], ACT.Abs)
         hid_codes = sb.tile([P, O], U32, name="hid_codes", align_bytes=64)
         hid_scales = sb.tile([P, O], U8, name="hid_scales", align_bytes=64)
         nc.vector.quantize_mx(hid_codes[:].bitcast(E5M2), hid_scales[:], hid_words[:].rearrange("p o t -> p (o t)"))
 
-        for t in range(PACK):
-            acc = psum.tile([P, O], F32, name="acc_p%d" % t)
-            nc.tensor.matmul_mx(
-                acc[:],
-                lhsT=wb_codes[:, 2 * P * t : 2 * P * (t + 1)].bitcast(E2M1),
-                lhsT_scale=wb_planes[:, t, :],
-                rhs=hid_codes[:].bitcast(E5M2),
-                rhs_scale=hid_scales[:],
-                start=True,
-                stop=True,
-            )
-            p_t = sb.tile([P, O], F32, name="p%d" % t)
-            if t == 0:
-                nc.vector.tensor_copy(p_t[:], acc[:])
-                nc.vector.tensor_copy(page[t][:].indirect(idx4[:]), p_t[:])
+        banks = ((0,), (1,), (2, 3))
+        p_rows = []
+        for bank, planes in enumerate(banks):
+            acc = psum.tile([P, len(planes), O], F32, name="acc_p%d" % bank)
+            for slot, t in enumerate(planes):
+                nc.tensor.matmul_mx(
+                    acc[:, slot, :],
+                    lhsT=wb_codes[:, 2 * P * t : 2 * P * (t + 1)].bitcast(E2M1),
+                    lhsT_scale=wb_planes[:, t, :],
+                    rhs=hid_codes[:].bitcast(E5M2),
+                    rhs_scale=hid_scales[:],
+                    start=True,
+                    stop=True,
+                )
+            p_sb = sb.tile([P, len(planes), O], F32, name="p%d" % bank)
+            if bank == 0:
+                nc.vector.tensor_copy(p_sb[:], acc[:])
             else:
-                nc.scalar.copy(p_t[:], acc[:])
-                nc.scalar.activation(page[t][:].indirect(idx4[:]), p_t[:], ACT.Copy)
+                nc.scalar.copy(p_sb[:], acc[:])
+            p_rows.extend(p_sb[:, slot, :] for slot in range(len(planes)))
+        nc.vector.tensor_copy(page[0][:].indirect(idx4[:]), p_rows[0])
+        for t in range(1, PACK):
+            nc.scalar.activation(page[t][:].indirect(idx4[:]), p_rows[t], ACT.Copy)
 
-        chunks = C // CHUNK
-        y = [sb.tile([P, PACK, CHUNK], F32, name="y%d" % c) for c in range(chunks)]
         out_rows = out_0.rearrange("(p t) c -> p t c", t=PACK)
         out_words = out_1[0].rearrange("p c t -> p (c t)").bitcast(I32)
         y_scales = sb.tile([P, C], U8, name="y_scales", align_bytes=64)
+        spans = [slice(sum(WIDTHS[:s]), sum(WIDTHS[: s + 1])) for s in range(len(WIDTHS))]
+        y = [sb.tile([P, PACK, width], F32, name="y%d" % s) for s, width in enumerate(WIDTHS)]
+        y_words = [
+            sb.tile([P, width, PACK], BF16, name="y_words%d" % s, align_bytes=64) for s, width in enumerate(WIDTHS)
+        ]
 
-        def add_pair(c, h):
-            cols = slice(c * CHUNK, (c + 1) * CHUNK)
-            for t in (2 * h, 2 * h + 1):
-                nc.vector.scalar_tensor_tensor(
-                    y[c][:, t, :], old_sb[t][:, cols], 0.5, page[t][:, cols], ALU.mult, ALU.add
-                )
-            nc.sync.dma_start(out_rows[:, 2 * h : 2 * h + 2, cols], y[c][:, 2 * h : 2 * h + 2, :])
-
-        y_words = [sb.tile([P, CHUNK, PACK], BF16, name="y_words%d" % c, align_bytes=64) for c in range(chunks)]
-
-        def weave(c):
-            dst = y_words[c][:].rearrange("p (c i) t -> p c t i", i=4)
-            src = y[c][:].rearrange("p t (c i) -> p c t i", i=4)
-            if c < chunks - 1:
-                nc.scalar.copy(dst, src)
-            else:
-                nc.scalar.copy(dst[:, :Y_SCALAR], src[:, :Y_SCALAR])
-                nc.vector.tensor_copy(dst[:, Y_SCALAR:], src[:, Y_SCALAR:])
-
-        def quantise(c):
-            cols = slice(c * CHUNK, (c + 1) * CHUNK)
-            y_codes = sb.tile([P, CHUNK], U32, name="y_codes%d" % c, align_bytes=64)
-            nc.vector.quantize_mx(
-                y_codes[:].bitcast(E4M3), y_scales[:, cols], y_words[c][:].rearrange("p c t -> p (c t)")
+        def add(s, t):
+            nc.vector.scalar_tensor_tensor(
+                y[s][:, t, :], old_sb[t][:, spans[s]], 0.5, page[t][:, spans[s]], ALU.mult, ALU.add
             )
-            nc.sync.dma_start(out_words[:, cols], y_codes[:].bitcast(I32))
 
-        for c in range(chunks - 1):
-            add_pair(c, 0)
-        for c in range(chunks - 1):
-            add_pair(c, 1)
-            weave(c)
+        def store(s, h):
+            nc.sync.dma_start(out_rows[:, 2 * h : 2 * h + 2, spans[s]], y[s][:, 2 * h : 2 * h + 2, :])
+
+        def quantise(s):
+            y_codes = sb.tile([P, WIDTHS[s]], U32, name="y_codes%d" % s, align_bytes=64)
+            nc.vector.quantize_mx(
+                y_codes[:].bitcast(E4M3), y_scales[:, spans[s]], y_words[s][:].rearrange("p c t -> p (c t)")
+            )
+            nc.sync.dma_start(out_words[:, spans[s]], y_codes[:].bitcast(I32))
+
+        last = len(WIDTHS) - 1
+        for s in range(len(WIDTHS)):
+            add(s, 0)
+        for s in range(len(WIDTHS)):
+            add(s, 1)
+            store(s, 0)
+        for s in range(last):
+            add(s, 2)
+        for s in range(len(WIDTHS)):
+            if s == last:
+                add(s, 2)
+            add(s, 3)
+            store(s, 1)
+            copy = nc.vector.tensor_copy if s == last else nc.scalar.copy
+            copy(
+                y_words[s][:].rearrange("p (c i) t -> p c t i", i=2),
+                y[s][:].rearrange("p t (c i) -> p c t i", i=2),
+            )
         quantise(0)
-        add_pair(chunks - 1, 0)
-        add_pair(chunks - 1, 1)
+        quantise(last)
         quantise(1)
-        weave(chunks - 1)
-        quantise(2)
-        quantise(3)
         for q in range(4):
             queue = nc.sync if q % 2 == 0 else nc.scalar
             queue.dma_start(out_2[0, 4 * q : 4 * q + 4, :].bitcast(I32), y_scales[32 * q : 32 * q + 4, :].bitcast(I32))

from contextlib import ExitStack

import concourse.mybir as mybir

K, T, J, B, R, O, N, C = 512, 512, 256, 32, 512, 128, 512, 1024
FLOPS = 2 * K * R * J + 2 * R * N * O

F32 = mybir.dt.float32
BF16 = mybir.dt.bfloat16
I32 = mybir.dt.int32
U32 = mybir.dt.uint32
U16 = mybir.dt.uint16
U8 = mybir.dt.uint8
E4M3 = mybir.dt.float8_e4m3fn_x4
E5M2 = mybir.dt.float8_e5m2_x4
E2M1 = mybir.dt.float4_e2m1fn_x4
ALU = mybir.AluOpType
ACT = mybir.ActivationFunctionType

P = 128
PACK = 4
GROUP = J // B
U_SCALAR = 28
WIDTHS = (256, 256, 512)


def tile_list_looks_centredpicks_farther_scattered_pl_kernel(
    tc, xf, fk, w_words, w_scales, wb_words, wb_scales, old, offs, offs2, offs3, offs4, out_0, out_1, out_2
):
    nc = tc.nc
    with ExitStack() as ctx:
        lists = ctx.enter_context(tc.tile_pool(name="lists", bufs=1))
        sb = ctx.enter_context(tc.tile_pool(name="sb", bufs=1))
        psum = ctx.enter_context(tc.psum_pool(name="psum", bufs=1))

        idx = lists.tile([P, J // 16], U16, name="idx")
        idx2 = lists.tile([P, O // 16], U16, name="idx2")
        idx3 = lists.tile([P, O // 16], U16, name="idx3")
        idx4 = lists.tile([P, O // 16], U16, name="idx4")

        w_scales_raw = sb.tile([P, R], U8, name="w_scales_raw", align_bytes=64)
        wb_scales_raw = sb.tile([P, N], U8, name="wb_scales_raw", align_bytes=64)
        nc.gpsimd.memset(w_scales_raw[:].bitcast(I32), 0)
        nc.gpsimd.memset(wb_scales_raw[:].bitcast(I32), 0)
        warm = sb.tile([P, 2], F32, name="warm")
        nc.gpsimd.memset(warm[:, 0:1], 0.0)
        nc.scalar.activation(warm[:, 1:2], warm[:, 0:1], ACT.Abs)
        page = [sb.tile([P, C], F32, name="page%d" % t) for t in range(PACK)]
        for t in range(PACK - 1):
            nc.vector.memset(page[t][:], 0.0)

        xf_rows = xf.rearrange("(p t) c -> p t c", t=PACK)
        x = [sb.tile([P, T], F32, name="x%d" % t, tag="tokens%d" % t) for t in range(PACK)]
        factor = sb.tile([P, PACK], F32, name="factor")
        w_raw = sb.tile([P, R], U32, name="w_raw")
        wb_raw = sb.tile([P, 2 * N], U8, name="wb_raw", tag="undealt_b", align_bytes=64)
        old_rows = old.rearrange("(p t) c -> p t c", t=PACK)

        for t in range(PACK):
            nc.sync.dma_start(x[t][:], xf_rows[:, t, :])
            if t == 0:
                nc.sync.dma_start(idx[:], offs)
                nc.sync.dma_start(factor[:], fk.rearrange("(p t) o -> p (t o)", t=PACK))
        nc.sync.dma_start(w_raw[:].bitcast(I32), w_words[0].rearrange("p n t -> p (n t)").bitcast(I32))
        for q in range(4):
            nc.sync.dma_start(
                w_scales_raw[32 * q : 32 * q + 4, :].bitcast(I32), w_scales[0, 4 * q : 4 * q + 4, :].bitcast(I32)
            )
        nc.sync.dma_start(wb_raw[:].bitcast(I32), wb_words[0].bitcast(I32))
        for q in range(4):
            nc.sync.dma_start(
                wb_scales_raw[32 * q : 32 * q + 4, :].bitcast(I32), wb_scales[0, 4 * q : 4 * q + 4, :].bitcast(I32)
            )
        nc.gpsimd.memset(page[PACK - 1][:], 0.0)
        nc.sync.dma_start(idx3[:], offs3)
        nc.sync.dma_start(idx2[:], offs2)
        nc.sync.dma_start(idx4[:], offs4)
        old_sb = [sb.tile([P, C], F32, name="old%d" % t) for t in range(PACK)]
        for t in range(PACK):
            nc.sync.dma_start(old_sb[t][:], old_rows[:, t, :])

        centred = []
        for t in range(PACK):
            xg = sb.tile([P, B, GROUP], F32, name="xg%d" % t, tag="picked%d" % t, align_bytes=64)
            nc.scalar.activation(xg[:].rearrange("p b i -> p (b i)"), x[t][:].indirect(idx[:]), ACT.Copy)
            sums = sb.tile([P, B], F32, name="sums%d" % t)
            nc.vector.tensor_reduce(sums[:], xg[:], mybir.AxisListType.X, ALU.add)
            centred_t = sb.tile([P, B, GROUP], F32, name="centred%d" % t)
            nc.vector.scalar_tensor_tensor(
                centred_t[:], sums[:].unsqueeze(2).to_broadcast([P, B, GROUP]), -1.0 / GROUP, xg[:], ALU.mult, ALU.add
            )
            centred.append(centred_t)
        u_planes = sb.tile([P, PACK, J], BF16, name="u_planes", tag="tokens%d" % (PACK - 1))
        for t in range(PACK):
            nc.scalar.activation(
                u_planes[:, t, :], centred[t][:].rearrange("p b i -> p (b i)"), ACT.Copy, scale=factor[:, t : t + 1]
            )

        w_codes = sb.tile([P, PACK, R // PACK], U32, name="w_codes", tag="picked%d" % (PACK - 2), align_bytes=64)
        nc.vector.tensor_copy(
            w_codes[:].rearrange("p t (m i) -> p m t i", i=4), w_raw[:].rearrange("p (m i t) -> p m t i", i=4, t=PACK)
        )

        w_planes = sb.tile([P, PACK, R // PACK], U8, name="w_planes", tag="picked%d" % (PACK - 1), align_bytes=64)
        nc.vector.tensor_copy(
            w_planes[:].rearrange("p t (m i) -> p m t i", i=16),
            w_scales_raw[:].rearrange("p (m i t) -> p m t i", i=16, t=PACK),
        )
        u_codes = sb.tile([P, J], U32, name="u_codes", align_bytes=64)
        u_scales = sb.tile([P, J], U8, name="u_scales", align_bytes=64)
        u_words = sb.tile([P, J, PACK], BF16, name="u_words", tag="woven", align_bytes=64)
        u_dst = u_words[:].rearrange("p (c i) t -> p c t i", i=4)
        u_src = u_planes[:].rearrange("p t (c i) -> p c t i", i=4)
        nc.scalar.copy(u_dst[:, :U_SCALAR], u_src[:, :U_SCALAR])
        nc.vector.tensor_copy(u_dst[:, U_SCALAR:], u_src[:, U_SCALAR:])
        nc.vector.quantize_mx(u_codes[:].bitcast(E4M3), u_scales[:], u_words[:].rearrange("p j t -> p (j t)"))

        wb_codes = sb.tile([P, 2 * N], U8, name="wb_codes", tag="woven", align_bytes=64)
        nc.vector.tensor_copy(
            wb_codes[:].bitcast(U16).rearrange("p (t m i) -> p m t i", t=PACK, i=8),
            wb_raw[:].bitcast(U16).rearrange("p (m i t) -> p m t i", t=PACK, i=8),
        )

        wb_planes = sb.tile([P, PACK, N // PACK], U8, name="wb_planes", tag="undealt_b", align_bytes=64)
        nc.vector.tensor_copy(
            wb_planes[:].rearrange("p t (m i) -> p m t i", i=16),
            wb_scales_raw[:].rearrange("p (m i t) -> p m t i", i=16, t=PACK),
        )

        a = []
        for t in range(PACK):
            acc = psum.tile([P, J], F32, name="acc_a%d" % t)
            nc.tensor.matmul_mx(
                acc[:],
                lhsT=w_codes[:, t, :].bitcast(E4M3),
                lhsT_scale=w_planes[:, t, :],
                rhs=u_codes[:].bitcast(E4M3),
                rhs_scale=u_scales[:],
                start=True,
                stop=True,
            )
            a_t = sb.tile([P, J], F32, name="a%d" % t)
            if t % 2 == 0:
                nc.scalar.copy(a_t[:], acc[:])
            else:
                nc.vector.tensor_copy(a_t[:], acc[:])
            a.append(a_t)
        diff = sb.tile([P, PACK, O], F32, name="diff")
        for t in range(PACK):
            half = sb.tile([P, O], F32, name="half%d" % t)
            nc.scalar.activation(half[:], a[t][:].indirect(idx3[:]), ACT.Copy, scale=-0.5)
            nc.vector.tensor_tensor(diff[:, t, :], a[t][:].indirect(idx2[:]), half[:], ALU.add)
        hid_words = sb.tile([P, O, PACK], BF16, name="hid_words", align_bytes=64)
        diff_words = diff[:].rearrange("p t o -> p o t")
        for h in range(2):
            pair = slice(2 * h, 2 * h + 2)
            nc.scalar.activation(hid_words[:, :, pair], diff_words[:, :, pair], ACT.Abs)
        hid_codes = sb.tile([P, O], U32, name="hid_codes", align_bytes=64)
        hid_scales = sb.tile([P, O], U8, name="hid_scales", align_bytes=64)
        nc.vector.quantize_mx(hid_codes[:].bitcast(E5M2), hid_scales[:], hid_words[:].rearrange("p o t -> p (o t)"))

        banks = ((0,), (1,), (2, 3))
        p_rows = []
        for bank, planes in enumerate(banks):
            acc = psum.tile([P, len(planes), O], F32, name="acc_p%d" % bank)
            for slot, t in enumerate(planes):
                nc.tensor.matmul_mx(
                    acc[:, slot, :],
                    lhsT=wb_codes[:, 2 * P * t : 2 * P * (t + 1)].bitcast(E2M1),
                    lhsT_scale=wb_planes[:, t, :],
                    rhs=hid_codes[:].bitcast(E5M2),
                    rhs_scale=hid_scales[:],
                    start=True,
                    stop=True,
                )
            p_sb = sb.tile([P, len(planes), O], F32, name="p%d" % bank)
            if bank == 0:
                nc.vector.tensor_copy(p_sb[:], acc[:])
            else:
                nc.scalar.copy(p_sb[:], acc[:])
            p_rows.extend(p_sb[:, slot, :] for slot in range(len(planes)))
        nc.vector.tensor_copy(page[0][:].indirect(idx4[:]), p_rows[0])
        for t in range(1, PACK):
            nc.scalar.activation(page[t][:].indirect(idx4[:]), p_rows[t], ACT.Copy)

        out_rows = out_0.rearrange("(p t) c -> p t c", t=PACK)
        out_words = out_1[0].rearrange("p c t -> p (c t)").bitcast(I32)
        y_scales = sb.tile([P, C], U8, name="y_scales", align_bytes=64)
        spans = [slice(sum(WIDTHS[:s]), sum(WIDTHS[: s + 1])) for s in range(len(WIDTHS))]
        y = [sb.tile([P, PACK, width], F32, name="y%d" % s) for s, width in enumerate(WIDTHS)]
        y_words = [
            sb.tile([P, width, PACK], BF16, name="y_words%d" % s, align_bytes=64) for s, width in enumerate(WIDTHS)
        ]

        def add(s, t):
            nc.vector.scalar_tensor_tensor(
                y[s][:, t, :], old_sb[t][:, spans[s]], 0.5, page[t][:, spans[s]], ALU.mult, ALU.add
            )

        def store(s, h):
            nc.sync.dma_start(out_rows[:, 2 * h : 2 * h + 2, spans[s]], y[s][:, 2 * h : 2 * h + 2, :])

        def quantise(s):
            y_codes = sb.tile([P, WIDTHS[s]], U32, name="y_codes%d" % s, align_bytes=64)
            nc.vector.quantize_mx(
                y_codes[:].bitcast(E4M3), y_scales[:, spans[s]], y_words[s][:].rearrange("p c t -> p (c t)")
            )
            nc.sync.dma_start(out_words[:, spans[s]], y_codes[:].bitcast(I32))

        last = len(WIDTHS) - 1
        for s in range(len(WIDTHS)):
            add(s, 0)
        for s in range(len(WIDTHS)):
            add(s, 1)
            store(s, 0)
        for s in range(last):
            add(s, 2)
        for s in range(len(WIDTHS)):
            if s == last:
                add(s, 2)
            add(s, 3)
            store(s, 1)
            copy = nc.vector.tensor_copy if s == last else nc.scalar.copy
            copy(
                y_words[s][:].rearrange("p (c i) t -> p c t i", i=2),
                y[s][:].rearrange("p t (c i) -> p c t i", i=2),
            )
        quantise(0)
        quantise(last)
        quantise(1)
        for q in range(4):
            queue = nc.sync if q % 2 == 0 else nc.scalar
            queue.dma_start(out_2[0, 4 * q : 4 * q + 4, :].bitcast(I32), y_scales[32 * q : 32 * q + 4, :].bitcast(I32))
